import numpy as np
import ml_dtypes


def mxq(x, axis, fmt="e4m3"):
    dtype, down = {"e4m3": (ml_dtypes.float8_e4m3fn, 7), "e5m2": (ml_dtypes.float8_e5m2, 14)}[fmt]
    v = np.moveaxis(np.asarray(x, np.float32).astype(ml_dtypes.bfloat16).astype(np.float64), axis, -1)
    blocks = v.reshape(v.shape[:-1] + (-1, 32))
    amax = np.abs(blocks).max(-1, keepdims=True)
    byte = np.maximum(np.where(amax > 0, np.frexp(amax)[1] - 1 + 127, 0) - down, 1)
    scale = np.exp2(byte - 127.0)
    codes = (blocks / scale).astype(np.float32).astype(dtype).astype(np.float64)
    return np.moveaxis((codes * scale).reshape(v.shape), -1, axis)


WIDE = False


def mx_kscale(k):
    if not WIDE:
        return np.ones(k)
    levels = np.array([30, -30])
    if k % 512:
        return np.exp2(np.random.permutation(np.resize(levels, k // 32))).repeat(32)
    a = np.empty((k // 512, 16))
    for p in range(k // 512):
        a[p, :8] = np.random.permutation(np.resize(levels, 8))
        for g in range(8):
            far = levels[np.abs(levels - a[p, g]) >= 10]
            a[p, g + 8] = far[np.random.randint(len(far))]
    return np.exp2(a.ravel()).repeat(32)


def f64(x):
    return np.asarray(x).astype(np.float64)


def striped(idx):
    return np.tile(np.asarray(idx).reshape(-1, 16).T, (8, 1)).astype(np.uint16)


def unstriped(offs):
    return offs[:16].T.reshape(-1).astype(np.int64)


E2M1 = np.array([0.0, 0.5, 1.0, 1.5, 2.0, 3.0, 4.0, 6.0, -0.0, -0.5, -1.0, -1.5, -2.0, -3.0, -4.0, -6.0])


def pack_weight(w, fmt):
    k, n = w.shape
    w = f64(np.asarray(w, np.float32).astype(ml_dtypes.bfloat16)).reshape(k // 32, 32, n)
    amax = np.abs(w).max(1)
    if fmt in ("e4m3", "e5m2"):
        byte = np.frexp(amax)[1] - 1 + 127 - (7 if fmt == "e4m3" else 14)
    else:
        mant, ex = np.frexp(amax / 6.0)
        byte = np.where(mant > 0.5, ex, ex - 1) + 127
    byte = np.clip(np.where(amax > 0, byte, 1), 1, 254)
    scaled = (w * np.exp2(127.0 - byte)[:, None, :]).reshape(k, n).astype(np.float32)
    by_word = np.ascontiguousarray(scaled.reshape(k // 512, 128, 4, n).transpose(0, 1, 3, 2))
    if fmt in ("e4m3", "e5m2"):
        words = by_word.astype(ml_dtypes.float8_e4m3fn if fmt == "e4m3" else ml_dtypes.float8_e5m2).view(np.uint8)
    else:
        c = by_word.astype(ml_dtypes.float4_e2m1fn).view(np.uint8) & 0xF
        words = (c[..., 0::2] | (c[..., 1::2] << 4)).reshape(k // 512, 128, 2 * n)
    return np.ascontiguousarray(words), np.ascontiguousarray(byte.astype(np.uint8).reshape(k // 512, 16, n))


def unpack_weight(words, scales, fmt):
    g, _, n = scales.shape
    words = np.ascontiguousarray(words).reshape(g, 128, n, -1)
    if fmt in ("e4m3", "e5m2"):
        vals = words.view(ml_dtypes.float8_e4m3fn if fmt == "e4m3" else ml_dtypes.float8_e5m2).astype(np.float64)
    else:
        nib = np.empty((g, 128, n, 4), np.uint8)
        nib[..., 0::2] = words & 0xF
        nib[..., 1::2] = words >> 4
        vals = E2M1[nib]
    vals = vals * np.repeat(np.exp2(scales.astype(np.float64) - 127.0), 8, axis=1)[..., None]
    return vals.transpose(0, 1, 3, 2).reshape(g * 512, n)


K, T, J, N, L = 1024, 1024, 256, 256, 512


def setup_inputs():
    n = np.random.standard_normal
    idx = np.random.permutation(T)[:J]
    fk = mx_kscale(K)
    fl = mx_kscale(L)
    xtp = pack_weight(n((K, T)) * np.random.uniform(0.4, 1.6, (1, T)) / fk[:, None], "e4m3")
    wap = pack_weight(n((K, N)) * 1 / np.sqrt(K) * fk[:, None], "e5m2")
    wbp = pack_weight(n((L, N)) * 1 / np.sqrt(L) * fl[:, None], "e5m2")
    return {
        "xt_words": xtp[0],
        "xt_scales": xtp[1],
        "wa_words": wap[0],
        "wa_scales": wap[1],
        "sx": (n((L, J)) * np.random.uniform(0.4, 1.6, (1, J)) / fl[:, None]).astype(np.float32),
        "wb_words": wbp[0],
        "wb_scales": wbp[1],
        "bi": (np.random.uniform(-0.6, 0.6, (1, N))).astype(np.float32),
        "offs": striped(idx),
    }


def reference(xt_words, xt_scales, wa_words, wa_scales, sx, wb_words, wb_scales, bi, offs):
    idx = unstriped(offs)
    xtu = unpack_weight(xt_words, xt_scales, "e4m3")
    wau = unpack_weight(wa_words, wa_scales, "e5m2")
    wbu = unpack_weight(wb_words, wb_scales, "e5m2")
    xtidxg = xtu[:, idx]
    a = xtidxg.T @ wau
    sxq = mxq(f64(sx), 0, "e5m2")
    b0 = sxq.T @ wbu
    b2 = b0 + f64(bi)
    pa = np.max(np.abs(a), axis=1, keepdims=True)
    pb = np.max(np.abs(b2), axis=1, keepdims=True)
    y = 0.3 * (a * pb - b2 * pa)
    return y

@@ -1,0 +1,154 @@
+from contextlib import ExitStack
+
+import concourse.mybir as mybir
+
+K, T, J, N, L = 1024, 1024, 256, 256, 512
+FLOPS = 2 * J * N * (K + L)
+
+F32 = mybir.dt.float32
+BF16 = mybir.dt.bfloat16
+I32 = mybir.dt.int32
+U32 = mybir.dt.uint32
+U16 = mybir.dt.uint16
+U8 = mybir.dt.uint8
+E4M3X4 = mybir.dt.float8_e4m3fn_x4
+E5M2X4 = mybir.dt.float8_e5m2_x4
+ALU = mybir.AluOpType
+COPY = mybir.ActivationFunctionType.Copy
+AXIS_X = mybir.AxisListType.X
+
+P = 128
+PACK = 4
+PASSES = K // (P * PACK)
+J_TILES = J // P
+
+
+def load_scale_rows(queue, plane, scales, q):
+    queue.dma_start(
+        out=plane[32 * q : 32 * q + 4, :, :].bitcast(I32),
+        in_=scales[:, 4 * q : 4 * q + 4, :].rearrange("z r c -> r z c").bitcast(I32),
+    )
+
+
+def words_of(words, z):
+    return words[z].rearrange("p c r -> p (c r)").bitcast(I32)
+
+
+def tile_list_rows_owninput_crosspeaks_kernel(
+    tc, xt_words, xt_scales, wa_words, wa_scales, sx, wb_words, wb_scales, bi, offs, out
+):
+    nc = tc.nc
+    with ExitStack() as ctx:
+        sb = ctx.enter_context(tc.tile_pool(name="sb", bufs=1))
+        ps = ctx.enter_context(tc.psum_pool(name="ps", bufs=1))
+
+        offsets = sb.tile([P, J // 16], U16, name="offsets")
+        xt_plane = sb.tile([P, PASSES, T], U8, name="xt_plane", align_bytes=64)
+        sx_raw = sb.tile([P, PACK, J], F32, name="sx_raw")
+        wb_plane = sb.tile([P, 1, N], U8, name="wb_plane", align_bytes=64)
+        wa_plane = sb.tile([P, PASSES, N], U8, name="wa_plane", align_bytes=64)
+        wb_codes = sb.tile([P, N], U32, name="wb_codes", align_bytes=64)
+        bias = sb.tile([P, N], F32, name="bias")
+        xt_table = [sb.tile([P, T], U32, name="xt_table%d" % z, align_bytes=64) for z in range(PASSES)]
+        wa_codes = sb.tile([P, PASSES, N], U32, name="wa_codes", align_bytes=64)
+
+        nc.vector.memset(xt_plane[:].rearrange("p z c -> p (z c)").bitcast(I32), 0)
+        nc.sync.dma_start(offsets[:], offs)
+        nc.sync.dma_start(out=sx_raw[:], in_=sx.rearrange("(p t) j -> p t j", t=PACK))
+        load_scale_rows(nc.sync, xt_plane, xt_scales, 0)
+        load_scale_rows(nc.sync, xt_plane, xt_scales, 1)
+        load_scale_rows(nc.sync, xt_plane, xt_scales, 2)
+        load_scale_rows(nc.sync, xt_plane, xt_scales, 3)
+        load_scale_rows(nc.scalar, wb_plane, wb_scales, 0)
+        load_scale_rows(nc.scalar, wb_plane, wb_scales, 1)
+        load_scale_rows(nc.gpsimd, wb_plane, wb_scales, 2)
+        load_scale_rows(nc.gpsimd, wb_plane, wb_scales, 3)
+        nc.sync.dma_start(out=wb_codes[:].bitcast(I32), in_=words_of(wb_words, 0))
+        nc.sync.dma_start(out=xt_table[0][:].bitcast(I32), in_=words_of(xt_words, 0))
+        nc.sync.dma_start(out=bias[:], in_=bi[0].partition_broadcast(P))
+        nc.sync.dma_start(out=xt_table[1][:].bitcast(I32), in_=words_of(xt_words, 1))
+        load_scale_rows(nc.sync, wa_plane, wa_scales, 0)
+        load_scale_rows(nc.sync, wa_plane, wa_scales, 1)
+        load_scale_rows(nc.sync, wa_plane, wa_scales, 2)
+        load_scale_rows(nc.sync, wa_plane, wa_scales, 3)
+        nc.sync.dma_start(out=wa_codes[:].bitcast(I32), in_=wa_words.rearrange("z p c r -> p z (c r)").bitcast(I32))
+
+        xg_plane = [sb.tile([P, J], U8, name="xg_plane%d" % z, align_bytes=64) for z in range(PASSES)]
+        for z in range(PASSES):
+            nc.vector.tensor_copy(xg_plane[z][:], xt_plane[:, z, :].indirect(offsets[:]))
+
+        sx_bf = sb.tile([P, J, PACK], BF16, name="sx_bf", align_bytes=64)
+        nc.scalar.copy(
+            sx_bf[:].rearrange("p (c i) t -> p c t i", i=4),
+            sx_raw[:].rearrange("p t (c i) -> p c t i", i=4),
+        )
+        sx_codes = sb.tile([P, J], U32, name="sx_codes", align_bytes=64)
+        sx_plane = sb.tile([P, J], U8, name="sx_plane", align_bytes=64)
+        nc.vector.quantize_mx(
+            out=sx_codes[:].bitcast(E5M2X4),
+            scales=sx_plane[:],
+            in_=sx_bf[:].rearrange("p j t -> p (j t)"),
+        )
+
+        xg_codes = [sb.tile([P, J], U32, name="xg_codes%d" % z, align_bytes=64) for z in range(PASSES)]
+        nc.vector.tensor_copy(xg_codes[0][:], xt_table[0][:].indirect(offsets[:]))
+
+        neg_b2 = []
+        peak_b = []
+        for h in range(J_TILES):
+            cols = slice(h * P, (h + 1) * P)
+            b0 = ps.tile([P, N], F32, name="b0_%d" % h)
+            nc.tensor.matmul_mx(
+                out=b0[:],
+                lhsT=sx_codes[:, cols].bitcast(E5M2X4),
+                lhsT_scale=sx_plane[:, cols],
+                rhs=wb_codes[:].bitcast(E5M2X4),
+                rhs_scale=wb_plane[:, 0, :],
+                start=True,
+                stop=True,
+            )
+            nb = sb.tile([P, N], F32, name="neg_b2_%d" % h)
+            nc.vector.scalar_tensor_tensor(
+                out=nb[:], in0=b0[:], scalar=-1.0, in1=bias[:], op0=ALU.mult, op1=ALU.subtract
+            )
+            neg_b2.append(nb)
+        for h in range(J_TILES):
+            pb = sb.tile([P, 1], F32, name="peak_b%d" % h)
+            nc.vector.tensor_reduce(out=pb[:], in_=neg_b2[h][:], axis=AXIS_X, op=ALU.max, apply_absolute_value=True)
+            peak_b.append(pb)
+
+        nc.vector.tensor_copy(xg_codes[1][:], xt_table[1][:].indirect(offsets[:]))
+
+        a_scaled = []
+        for h in range(J_TILES):
+            cols = slice(h * P, (h + 1) * P)
+            a = ps.tile([P, N], F32, name="a_%d" % h)
+            for z in range(PASSES):
+                nc.tensor.matmul_mx(
+                    out=a[:],
+                    lhsT=xg_codes[z][:, cols].bitcast(E4M3X4),
+                    lhsT_scale=xg_plane[z][:, cols],
+                    rhs=wa_codes[:, z, :].bitcast(E5M2X4),
+                    rhs_scale=wa_plane[:, z, :],
+                    start=(z == 0),
+                    stop=(z == PASSES - 1),
+                )
+            c = sb.tile([P, N], F32, name="a_scaled%d" % h)
+            nc.scalar.activation(c[:], a[:], COPY, scale=0.3)
+            a_scaled.append(c)
+
+        peak_a = []
+        first = []
+        for h in range(J_TILES):
+            pa = sb.tile([P, 1], F32, name="peak_a%d" % h)
+            nc.vector.tensor_reduce(out=pa[:], in_=a_scaled[h][:], axis=AXIS_X, op=ALU.max, apply_absolute_value=True)
+            peak_a.append(pa)
+            f = sb.tile([P, N], F32, name="first%d" % h)
+            nc.scalar.activation(f[:], a_scaled[h][:], COPY, scale=peak_b[h][:])
+            first.append(f)
+        for h in range(J_TILES):
+            y = sb.tile([P, N], F32, name="y%d" % h)
+            nc.vector.scalar_tensor_tensor(
+                out=y[:], in0=neg_b2[h][:], scalar=peak_a[h][:], in1=first[h][:], op0=ALU.mult, op1=ALU.add
+            )
+            nc.sync.dma_start(out=out[h * P : (h + 1) * P, :], in_=y[:])

@@ -1,6 +1,7 @@
 from contextlib import ExitStack
 
 import concourse.mybir as mybir
+from concourse.masks import make_identity
 
 K, T, J, N, L = 1024, 1024, 256, 256, 512
 FLOPS = 2 * J * N * (K + L)
@@ -23,10 +24,10 @@ PASSES = K // (P * PACK)
 J_TILES = J // P
 
 
-def load_scale_rows(queue, plane, scales, q):
+def load_scale_rows(queue, plane, scales, r):
     queue.dma_start(
-        out=plane[32 * q : 32 * q + 4, :, :].bitcast(I32),
-        in_=scales[:, 4 * q : 4 * q + 4, :].rearrange("z r c -> r z c").bitcast(I32),
+        out=plane[r:P:32, :, :].bitcast(I32),
+        in_=scales[:, r:16:4, :].rearrange("z q c -> q z c").bitcast(I32),
     )
 
 
@@ -49,33 +50,41 @@ def tile_list_rows_owninput_crosspeaks_kernel(
         wa_plane = sb.tile([P, PASSES, N], U8, name="wa_plane", align_bytes=64)
         wb_codes = sb.tile([P, N], U32, name="wb_codes", align_bytes=64)
         bias = sb.tile([P, N], F32, name="bias")
+        bias_pairs = sb.tile([P, 2], F32, name="bias_pairs")
+        identity = sb.tile([P, P], F32, name="identity")
         xt_table = [sb.tile([P, T], U32, name="xt_table%d" % z, align_bytes=64) for z in range(PASSES)]
         wa_codes = sb.tile([P, PASSES, N], U32, name="wa_codes", align_bytes=64)
 
         nc.vector.memset(xt_plane[:].rearrange("p z c -> p (z c)").bitcast(I32), 0)
+        make_identity(nc, identity[:])
         nc.sync.dma_start(offsets[:], offs)
         nc.sync.dma_start(out=sx_raw[:], in_=sx.rearrange("(p t) j -> p t j", t=PACK))
         load_scale_rows(nc.sync, xt_plane, xt_scales, 0)
         load_scale_rows(nc.sync, xt_plane, xt_scales, 1)
         load_scale_rows(nc.sync, xt_plane, xt_scales, 2)
         load_scale_rows(nc.sync, xt_plane, xt_scales, 3)
-        load_scale_rows(nc.scalar, wb_plane, wb_scales, 0)
-        load_scale_rows(nc.scalar, wb_plane, wb_scales, 1)
-        load_scale_rows(nc.gpsimd, wb_plane, wb_scales, 2)
-        load_scale_rows(nc.gpsimd, wb_plane, wb_scales, 3)
+        nc.scalar.dma_start(out=bias_pairs[:], in_=bi[0].rearrange("(p c) -> p c", c=2))
         nc.sync.dma_start(out=wb_codes[:].bitcast(I32), in_=words_of(wb_words, 0))
         nc.sync.dma_start(out=xt_table[0][:].bitcast(I32), in_=words_of(xt_words, 0))
-        nc.sync.dma_start(out=bias[:], in_=bi[0].partition_broadcast(P))
+        load_scale_rows(nc.sync, wb_plane, wb_scales, 0)
+        load_scale_rows(nc.sync, wb_plane, wb_scales, 1)
+        load_scale_rows(nc.sync, wb_plane, wb_scales, 2)
+        load_scale_rows(nc.sync, wb_plane, wb_scales, 3)
+        nc.sync.dma_start(out=wa_codes[:].bitcast(I32), in_=wa_words.rearrange("z p c r -> p z (c r)").bitcast(I32))
         nc.sync.dma_start(out=xt_table[1][:].bitcast(I32), in_=words_of(xt_words, 1))
         load_scale_rows(nc.sync, wa_plane, wa_scales, 0)
-        load_scale_rows(nc.sync, wa_plane, wa_scales, 1)
-        load_scale_rows(nc.sync, wa_plane, wa_scales, 2)
-        load_scale_rows(nc.sync, wa_plane, wa_scales, 3)
-        nc.sync.dma_start(out=wa_codes[:].bitcast(I32), in_=wa_words.rearrange("z p c r -> p z (c r)").bitcast(I32))
+        load_scale_rows(nc.gpsimd, wa_plane, wa_scales, 1)
+        load_scale_rows(nc.gpsimd, wa_plane, wa_scales, 2)
+        load_scale_rows(nc.gpsimd, wa_plane, wa_scales, 3)
 
         xg_plane = [sb.tile([P, J], U8, name="xg_plane%d" % z, align_bytes=64) for z in range(PASSES)]
         for z in range(PASSES):
             nc.vector.tensor_copy(xg_plane[z][:], xt_plane[:, z, :].indirect(offsets[:]))
+
+        bias_rows = ps.tile([P, 2, P], F32, name="bias_rows")
+        for c in range(2):
+            nc.tensor.transpose(bias_rows[:, c, :], bias_pairs[:, c : c + 1].to_broadcast([P, P]), identity[:])
+        nc.scalar.copy(bias[:].rearrange("p (m c) -> p m c", c=2), bias_rows[:].rearrange("p c m -> p m c"))
 
         sx_bf = sb.tile([P, J, PACK], BF16, name="sx_bf", align_bytes=64)
         nc.scalar.copy(
@@ -90,8 +99,8 @@ def tile_list_rows_owninput_crosspeaks_kernel(
             in_=sx_bf[:].rearrange("p j t -> p (j t)"),
         )
 
-        xg_codes = [sb.tile([P, J], U32, name="xg_codes%d" % z, align_bytes=64) for z in range(PASSES)]
-        nc.vector.tensor_copy(xg_codes[0][:], xt_table[0][:].indirect(offsets[:]))
+        xg_first = sb.tile([P, J], U32, name="xg_first", align_bytes=64)
+        nc.vector.tensor_copy(xg_first[:], xt_table[0][:].indirect(offsets[:]))
 
         neg_b2 = []
         peak_b = []
@@ -117,24 +126,28 @@ def tile_list_rows_owninput_crosspeaks_kernel(
             nc.vector.tensor_reduce(out=pb[:], in_=neg_b2[h][:], axis=AXIS_X, op=ALU.max, apply_absolute_value=True)
             peak_b.append(pb)
 
-        nc.vector.tensor_copy(xg_codes[1][:], xt_table[1][:].indirect(offsets[:]))
+        acc = [ps.tile([P, N], F32, name="a_%d" % h) for h in range(J_TILES)]
 
+        def a_pass(h, z, codes):
+            nc.tensor.matmul_mx(
+                out=acc[h][:],
+                lhsT=codes.bitcast(E4M3X4),
+                lhsT_scale=xg_plane[z][:, h * P : (h + 1) * P],
+                rhs=wa_codes[:, z, :].bitcast(E5M2X4),
+                rhs_scale=wa_plane[:, z, :],
+                start=(z == 0),
+                stop=(z == PASSES - 1),
+            )
+
+        for h in range(J_TILES):
+            a_pass(h, 0, xg_first[:, h * P : (h + 1) * P])
         a_scaled = []
         for h in range(J_TILES):
-            cols = slice(h * P, (h + 1) * P)
-            a = ps.tile([P, N], F32, name="a_%d" % h)
-            for z in range(PASSES):
-                nc.tensor.matmul_mx(
-                    out=a[:],
-                    lhsT=xg_codes[z][:, cols].bitcast(E4M3X4),
-                    lhsT_scale=xg_plane[z][:, cols],
-                    rhs=wa_codes[:, z, :].bitcast(E5M2X4),
-                    rhs_scale=wa_plane[:, z, :],
-                    start=(z == 0),
-                    stop=(z == PASSES - 1),
-                )
+            xg_last = sb.tile([P, P], U32, name="xg_last%d" % h, align_bytes=64)
+            nc.vector.tensor_copy(xg_last[:], xt_table[1][:].indirect(offsets[:, 8 * h : 8 * (h + 1)]))
+            a_pass(h, 1, xg_last[:])
             c = sb.tile([P, N], F32, name="a_scaled%d" % h)
-            nc.scalar.activation(c[:], a[:], COPY, scale=0.3)
+            nc.scalar.activation(c[:], acc[h][:], COPY, scale=0.3)
             a_scaled.append(c)
 
         peak_a = []

@@ -56,7 +56,6 @@ def tile_list_rows_owninput_crosspeaks_kernel(
         wa_codes = sb.tile([P, PASSES, N], U32, name="wa_codes", align_bytes=64)
 
         nc.vector.memset(xt_plane[:].rearrange("p z c -> p (z c)").bitcast(I32), 0)
-        make_identity(nc, identity[:])
         nc.sync.dma_start(offsets[:], offs)
         nc.sync.dma_start(out=sx_raw[:], in_=sx.rearrange("(p t) j -> p t j", t=PACK))
         load_scale_rows(nc.sync, xt_plane, xt_scales, 0)
@@ -64,18 +63,19 @@ def tile_list_rows_owninput_crosspeaks_kernel(
         load_scale_rows(nc.sync, xt_plane, xt_scales, 2)
         load_scale_rows(nc.sync, xt_plane, xt_scales, 3)
         nc.scalar.dma_start(out=bias_pairs[:], in_=bi[0].rearrange("(p c) -> p c", c=2))
-        nc.sync.dma_start(out=wb_codes[:].bitcast(I32), in_=words_of(wb_words, 0))
         nc.sync.dma_start(out=xt_table[0][:].bitcast(I32), in_=words_of(xt_words, 0))
+        load_scale_rows(nc.sync, wa_plane, wa_scales, 0)
+        nc.sync.dma_start(out=xt_table[1][:].bitcast(I32), in_=words_of(xt_words, 1))
+        nc.sync.dma_start(out=wb_codes[:].bitcast(I32), in_=words_of(wb_words, 0))
         load_scale_rows(nc.sync, wb_plane, wb_scales, 0)
         load_scale_rows(nc.sync, wb_plane, wb_scales, 1)
         load_scale_rows(nc.sync, wb_plane, wb_scales, 2)
         load_scale_rows(nc.sync, wb_plane, wb_scales, 3)
+        load_scale_rows(nc.sync, wa_plane, wa_scales, 1)
         nc.sync.dma_start(out=wa_codes[:].bitcast(I32), in_=wa_words.rearrange("z p c r -> p z (c r)").bitcast(I32))
-        nc.sync.dma_start(out=xt_table[1][:].bitcast(I32), in_=words_of(xt_words, 1))
-        load_scale_rows(nc.sync, wa_plane, wa_scales, 0)
-        load_scale_rows(nc.gpsimd, wa_plane, wa_scales, 1)
         load_scale_rows(nc.gpsimd, wa_plane, wa_scales, 2)
         load_scale_rows(nc.gpsimd, wa_plane, wa_scales, 3)
+        make_identity(nc, identity[:])
 
         xg_plane = [sb.tile([P, J], U8, name="xg_plane%d" % z, align_bytes=64) for z in range(PASSES)]
         for z in range(PASSES):
@@ -99,8 +99,9 @@ def tile_list_rows_owninput_crosspeaks_kernel(
             in_=sx_bf[:].rearrange("p j t -> p (j t)"),
         )
 
-        xg_first = sb.tile([P, J], U32, name="xg_first", align_bytes=64)
-        nc.vector.tensor_copy(xg_first[:], xt_table[0][:].indirect(offsets[:]))
+        xg_codes = [sb.tile([P, J], U32, name="xg_codes%d" % z, align_bytes=64) for z in range(PASSES)]
+        for z in range(PASSES):
+            nc.vector.tensor_copy(xg_codes[z][:], xt_table[z][:].indirect(offsets[:]))
 
         neg_b2 = []
         peak_b = []
@@ -126,28 +127,22 @@ def tile_list_rows_owninput_crosspeaks_kernel(
             nc.vector.tensor_reduce(out=pb[:], in_=neg_b2[h][:], axis=AXIS_X, op=ALU.max, apply_absolute_value=True)
             peak_b.append(pb)
 
-        acc = [ps.tile([P, N], F32, name="a_%d" % h) for h in range(J_TILES)]
-
-        def a_pass(h, z, codes):
-            nc.tensor.matmul_mx(
-                out=acc[h][:],
-                lhsT=codes.bitcast(E4M3X4),
-                lhsT_scale=xg_plane[z][:, h * P : (h + 1) * P],
-                rhs=wa_codes[:, z, :].bitcast(E5M2X4),
-                rhs_scale=wa_plane[:, z, :],
-                start=(z == 0),
-                stop=(z == PASSES - 1),
-            )
-
-        for h in range(J_TILES):
-            a_pass(h, 0, xg_first[:, h * P : (h + 1) * P])
         a_scaled = []
         for h in range(J_TILES):
-            xg_last = sb.tile([P, P], U32, name="xg_last%d" % h, align_bytes=64)
-            nc.vector.tensor_copy(xg_last[:], xt_table[1][:].indirect(offsets[:, 8 * h : 8 * (h + 1)]))
-            a_pass(h, 1, xg_last[:])
+            cols = slice(h * P, (h + 1) * P)
+            a = ps.tile([P, N], F32, name="a_%d" % h)
+            for z in range(PASSES):
+                nc.tensor.matmul_mx(
+                    out=a[:],
+                    lhsT=xg_codes[z][:, cols].bitcast(E4M3X4),
+                    lhsT_scale=xg_plane[z][:, cols],
+                    rhs=wa_codes[:, z, :].bitcast(E5M2X4),
+                    rhs_scale=wa_plane[:, z, :],
+                    start=(z == 0),
+                    stop=(z == PASSES - 1),
+                )
             c = sb.tile([P, N], F32, name="a_scaled%d" % h)
-            nc.scalar.activation(c[:], acc[h][:], COPY, scale=0.3)
+            nc.scalar.activation(c[:], a[:], COPY, scale=0.3)
             a_scaled.append(c)
 
         peak_a = []

from contextlib import ExitStack

import concourse.mybir as mybir
from concourse.masks import make_identity

K, T, J, N, L = 1024, 1024, 256, 256, 512
FLOPS = 2 * J * N * (K + L)

F32 = mybir.dt.float32
BF16 = mybir.dt.bfloat16
I32 = mybir.dt.int32
U32 = mybir.dt.uint32
U16 = mybir.dt.uint16
U8 = mybir.dt.uint8
E4M3X4 = mybir.dt.float8_e4m3fn_x4
E5M2X4 = mybir.dt.float8_e5m2_x4
ALU = mybir.AluOpType
COPY = mybir.ActivationFunctionType.Copy
AXIS_X = mybir.AxisListType.X

P = 128
PACK = 4
PASSES = K // (P * PACK)
J_TILES = J // P


def load_scale_rows(queue, plane, scales, r):
    queue.dma_start(
        out=plane[r:P:32, :, :].bitcast(I32),
        in_=scales[:, r:16:4, :].rearrange("z q c -> q z c").bitcast(I32),
    )


def words_of(words, z):
    return words[z].rearrange("p c r -> p (c r)").bitcast(I32)


def tile_list_rows_owninput_crosspeaks_kernel(
    tc, xt_words, xt_scales, wa_words, wa_scales, sx, wb_words, wb_scales, bi, offs, out
):
    nc = tc.nc
    with ExitStack() as ctx:
        sb = ctx.enter_context(tc.tile_pool(name="sb", bufs=1))
        ps = ctx.enter_context(tc.psum_pool(name="ps", bufs=1))

        offsets = sb.tile([P, J // 16], U16, name="offsets")
        xt_plane = sb.tile([P, PASSES, T], U8, name="xt_plane", align_bytes=64)
        sx_raw = sb.tile([P, PACK, J], F32, name="sx_raw")
        wb_plane = sb.tile([P, 1, N], U8, name="wb_plane", align_bytes=64)
        wa_plane = sb.tile([P, PASSES, N], U8, name="wa_plane", align_bytes=64)
        wb_codes = sb.tile([P, N], U32, name="wb_codes", align_bytes=64)
        bias = sb.tile([P, N], F32, name="bias")
        bias_pairs = sb.tile([P, 2], F32, name="bias_pairs")
        identity = sb.tile([P, P], F32, name="identity")
        xt_table = [sb.tile([P, T], U32, name="xt_table%d" % z, align_bytes=64) for z in range(PASSES)]
        wa_codes = sb.tile([P, PASSES, N], U32, name="wa_codes", align_bytes=64)

        nc.vector.memset(xt_plane[:].rearrange("p z c -> p (z c)").bitcast(I32), 0)
        nc.sync.dma_start(offsets[:], offs)
        nc.sync.dma_start(out=sx_raw[:], in_=sx.rearrange("(p t) j -> p t j", t=PACK))
        load_scale_rows(nc.sync, xt_plane, xt_scales, 0)
        load_scale_rows(nc.sync, xt_plane, xt_scales, 1)
        load_scale_rows(nc.sync, xt_plane, xt_scales, 2)
        load_scale_rows(nc.sync, xt_plane, xt_scales, 3)
        nc.scalar.dma_start(out=bias_pairs[:], in_=bi[0].rearrange("(p c) -> p c", c=2))
        nc.sync.dma_start(out=xt_table[0][:].bitcast(I32), in_=words_of(xt_words, 0))
        load_scale_rows(nc.sync, wa_plane, wa_scales, 0)
        nc.sync.dma_start(out=xt_table[1][:].bitcast(I32), in_=words_of(xt_words, 1))
        nc.sync.dma_start(out=wb_codes[:].bitcast(I32), in_=words_of(wb_words, 0))
        load_scale_rows(nc.sync, wb_plane, wb_scales, 0)
        load_scale_rows(nc.sync, wb_plane, wb_scales, 1)
        load_scale_rows(nc.sync, wb_plane, wb_scales, 2)
        load_scale_rows(nc.sync, wb_plane, wb_scales, 3)
        load_scale_rows(nc.sync, wa_plane, wa_scales, 1)
        nc.sync.dma_start(out=wa_codes[:].bitcast(I32), in_=wa_words.rearrange("z p c r -> p z (c r)").bitcast(I32))
        load_scale_rows(nc.gpsimd, wa_plane, wa_scales, 2)
        load_scale_rows(nc.gpsimd, wa_plane, wa_scales, 3)
        make_identity(nc, identity[:])

        xg_plane = [sb.tile([P, J], U8, name="xg_plane%d" % z, align_bytes=64) for z in range(PASSES)]
        for z in range(PASSES):
            nc.vector.tensor_copy(xg_plane[z][:], xt_plane[:, z, :].indirect(offsets[:]))

        bias_rows = ps.tile([P, 2, P], F32, name="bias_rows")
        for c in range(2):
            nc.tensor.transpose(bias_rows[:, c, :], bias_pairs[:, c : c + 1].to_broadcast([P, P]), identity[:])
        nc.scalar.copy(bias[:].rearrange("p (m c) -> p m c", c=2), bias_rows[:].rearrange("p c m -> p m c"))

        sx_bf = sb.tile([P, J, PACK], BF16, name="sx_bf", align_bytes=64)
        nc.scalar.copy(
            sx_bf[:].rearrange("p (c i) t -> p c t i", i=4),
            sx_raw[:].rearrange("p t (c i) -> p c t i", i=4),
        )
        sx_codes = sb.tile([P, J], U32, name="sx_codes", align_bytes=64)
        sx_plane = sb.tile([P, J], U8, name="sx_plane", align_bytes=64)
        nc.vector.quantize_mx(
            out=sx_codes[:].bitcast(E5M2X4),
            scales=sx_plane[:],
            in_=sx_bf[:].rearrange("p j t -> p (j t)"),
        )

        xg_codes = [sb.tile([P, J], U32, name="xg_codes%d" % z, align_bytes=64) for z in range(PASSES)]
        for z in range(PASSES):
            nc.vector.tensor_copy(xg_codes[z][:], xt_table[z][:].indirect(offsets[:]))

        neg_b2 = []
        peak_b = []
        for h in range(J_TILES):
            cols = slice(h * P, (h + 1) * P)
            b0 = ps.tile([P, N], F32, name="b0_%d" % h)
            nc.tensor.matmul_mx(
                out=b0[:],
                lhsT=sx_codes[:, cols].bitcast(E5M2X4),
                lhsT_scale=sx_plane[:, cols],
                rhs=wb_codes[:].bitcast(E5M2X4),
                rhs_scale=wb_plane[:, 0, :],
                start=True,
                stop=True,
            )
            nb = sb.tile([P, N], F32, name="neg_b2_%d" % h)
            nc.vector.scalar_tensor_tensor(
                out=nb[:], in0=b0[:], scalar=-1.0, in1=bias[:], op0=ALU.mult, op1=ALU.subtract
            )
            neg_b2.append(nb)
        for h in range(J_TILES):
            pb = sb.tile([P, 1], F32, name="peak_b%d" % h)
            nc.vector.tensor_reduce(out=pb[:], in_=neg_b2[h][:], axis=AXIS_X, op=ALU.max, apply_absolute_value=True)
            peak_b.append(pb)

        a_scaled = []
        for h in range(J_TILES):
            cols = slice(h * P, (h + 1) * P)
            a = ps.tile([P, N], F32, name="a_%d" % h)
            for z in range(PASSES):
                nc.tensor.matmul_mx(
                    out=a[:],
                    lhsT=xg_codes[z][:, cols].bitcast(E4M3X4),
                    lhsT_scale=xg_plane[z][:, cols],
                    rhs=wa_codes[:, z, :].bitcast(E5M2X4),
                    rhs_scale=wa_plane[:, z, :],
                    start=(z == 0),
                    stop=(z == PASSES - 1),
                )
            c = sb.tile([P, N], F32, name="a_scaled%d" % h)
            nc.scalar.activation(c[:], a[:], COPY, scale=0.3)
            a_scaled.append(c)

        peak_a = []
        first = []
        for h in range(J_TILES):
            pa = sb.tile([P, 1], F32, name="peak_a%d" % h)
            nc.vector.tensor_reduce(out=pa[:], in_=a_scaled[h][:], axis=AXIS_X, op=ALU.max, apply_absolute_value=True)
            peak_a.append(pa)
            f = sb.tile([P, N], F32, name="first%d" % h)
            nc.scalar.activation(f[:], a_scaled[h][:], COPY, scale=peak_b[h][:])
            first.append(f)
        for h in range(J_TILES):
            y = sb.tile([P, N], F32, name="y%d" % h)
            nc.vector.scalar_tensor_tensor(
                out=y[:], in0=neg_b2[h][:], scalar=peak_a[h][:], in1=first[h][:], op0=ALU.mult, op1=ALU.add
            )
            nc.sync.dma_start(out=out[h * P : (h + 1) * P, :], in_=y[:])
